import numpy as np
import ml_dtypes


def mxq(x, axis, fmt="e4m3"):
    dtype, down = {"e4m3": (ml_dtypes.float8_e4m3fn, 7), "e5m2": (ml_dtypes.float8_e5m2, 14)}[fmt]
    v = np.moveaxis(np.asarray(x, np.float32).astype(ml_dtypes.bfloat16).astype(np.float64), axis, -1)
    blocks = v.reshape(v.shape[:-1] + (-1, 32))
    amax = np.abs(blocks).max(-1, keepdims=True)
    byte = np.maximum(np.where(amax > 0, np.frexp(amax)[1] - 1 + 127, 0) - down, 1)
    scale = np.exp2(byte - 127.0)
    codes = (blocks / scale).astype(np.float32).astype(dtype).astype(np.float64)
    return np.moveaxis((codes * scale).reshape(v.shape), -1, axis)


WIDE = False


def mx_kscale(k):
    if not WIDE:
        return np.ones(k)
    levels = np.array([10, -10, 5, -5, 0])
    if k % 512:
        return np.exp2(np.random.permutation(np.resize(levels, k // 32))).repeat(32)
    a = np.empty((k // 512, 16))
    for p in range(k // 512):
        a[p, :8] = np.random.permutation(np.resize(levels, 8))
        for g in range(8):
            far = levels[np.abs(levels - a[p, g]) >= 10]
            a[p, g + 8] = far[np.random.randint(len(far))]
    return np.exp2(a.ravel()).repeat(32)


def f64(x):
    return np.asarray(x).astype(np.float64)


def striped(idx):
    return np.tile(np.asarray(idx).reshape(-1, 16).T, (8, 1)).astype(np.uint16)


def unstriped(offs):
    return offs[:16].T.reshape(-1).astype(np.int64)


def striped8(idx):
    return np.asarray(idx).reshape(8, -1, 16).transpose(0, 2, 1).reshape(128, -1).astype(np.uint16)


def unstriped8(offs):
    return offs.reshape(8, 16, -1).transpose(0, 2, 1).reshape(8, -1).astype(np.int64)


def pick8(x, idx, run):
    r = np.arange(len(x))
    return x[r[:, None], idx[r % (8 * run) // run]]


E2M1 = np.array([0.0, 0.5, 1.0, 1.5, 2.0, 3.0, 4.0, 6.0, -0.0, -0.5, -1.0, -1.5, -2.0, -3.0, -4.0, -6.0])


def pack_weight(w, fmt):
    k, n = w.shape
    w = f64(np.asarray(w, np.float32).astype(ml_dtypes.bfloat16)).reshape(k // 32, 32, n)
    amax = np.abs(w).max(1)
    if fmt == "e4m3":
        byte = np.frexp(amax)[1] - 1 + 127 - 7
    else:
        mant, ex = np.frexp(amax / 6.0)
        byte = np.where(mant > 0.5, ex, ex - 1) + 127
    byte = np.clip(np.where(amax > 0, byte, 1), 1, 254)
    scaled = (w * np.exp2(127.0 - byte)[:, None, :]).reshape(k, n).astype(np.float32)
    by_word = np.ascontiguousarray(scaled.reshape(k // 512, 128, 4, n).transpose(0, 1, 3, 2))
    if fmt == "e4m3":
        words = by_word.astype(ml_dtypes.float8_e4m3fn).view(np.uint8)
    else:
        c = by_word.astype(ml_dtypes.float4_e2m1fn).view(np.uint8) & 0xF
        words = (c[..., 0::2] | (c[..., 1::2] << 4)).reshape(k // 512, 128, 2 * n)
    return np.ascontiguousarray(words), np.ascontiguousarray(byte.astype(np.uint8).reshape(k // 512, 16, n))


def unpack_weight(words, scales, fmt):
    g, _, n = scales.shape
    words = np.ascontiguousarray(words).reshape(g, 128, n, -1)
    if fmt == "e4m3":
        vals = words.view(ml_dtypes.float8_e4m3fn).astype(np.float64)
    else:
        nib = np.empty((g, 128, n, 4), np.uint8)
        nib[..., 0::2] = words & 0xF
        nib[..., 1::2] = words >> 4
        vals = E2M1[nib]
    vals = vals * np.repeat(np.exp2(scales.astype(np.float64) - 127.0), 8, axis=1)[..., None]
    return vals.transpose(0, 1, 3, 2).reshape(g * 512, n)


K, J, R, T, F, C, S, N = 512, 512, 512, 1024, 1024, 1024, 256, 256


def setup_inputs():
    n = np.random.standard_normal
    idx = np.random.permutation(T)[:J]
    idx2 = np.random.permutation(F)[:R]
    idx3 = np.stack([np.random.permutation(C)[:J] for _ in range(8)])
    idx4 = np.stack([np.random.permutation(J)[:S] for _ in range(8)])
    idx5 = np.stack([np.random.permutation(C)[:S] for _ in range(8)])
    idx6 = np.random.permutation(T)[:C]
    fk = mx_kscale(K)
    fr = mx_kscale(R)
    tr = np.ones(F)
    tr[idx2] = fr
    xtp = pack_weight(n((K, T)) * fk[:, None], "e4m3")
    wtp = pack_weight(n((K, F)) * 1 / np.sqrt(K) / fk[:, None] * tr, "e2m1")
    wbp = pack_weight(n((R, N)) * 1 / np.sqrt(R) / fr[:, None], "e4m3")
    wsp = pack_weight(n((K, N)) * 1 / np.sqrt(K) / fk[:, None], "e2m1")
    return {
        "xt_words": xtp[0],
        "xt_scales": xtp[1],
        "wt_words": wtp[0],
        "wt_scales": wtp[1],
        "sa": (np.random.uniform(0.5, 1.6, (R, 1))).astype(np.float32),
        "wb_words": wbp[0],
        "wb_scales": wbp[1],
        "ws_words": wsp[0],
        "ws_scales": wsp[1],
        "offs": striped(idx),
        "offs2": striped(idx2),
        "offs3": striped8(idx3),
        "offs4": striped8(idx4),
        "offs5": striped8(idx5),
        "offs6": striped(idx6),
    }


def reference(xt_words, xt_scales, wt_words, wt_scales, sa, wb_words, wb_scales, ws_words, ws_scales, offs, offs2, offs3, offs4, offs5, offs6):
    idx = unstriped(offs)
    idx2 = unstriped(offs2)
    idx3 = unstriped8(offs3)
    idx4 = unstriped8(offs4)
    idx5 = unstriped8(offs5)
    idx6 = unstriped(offs6)
    xtu = unpack_weight(xt_words, xt_scales, "e4m3")
    wtu = unpack_weight(wt_words, wt_scales, "e2m1")
    wbu = unpack_weight(wb_words, wb_scales, "e4m3")
    wsu = unpack_weight(ws_words, ws_scales, "e2m1")
    wtidx2g = wtu[:, idx2]
    xtidxg = xtu[:, idx]
    a = wtidx2g.T @ xtidxg
    pw = np.zeros((R, C))
    pw[np.arange(R)[:, None], idx3[np.arange(R) % 512 // 64]] = a
    h1 = pick8(a, idx4, 64) * f64(sa)
    pv = np.zeros((R, C))
    pv[np.arange(R)[:, None], idx5[np.arange(R) % 512 // 64]] = h1
    hid = np.abs(pw - pv)
    hidq = mxq(hid, 0, "e4m3")
    xtidx6g = xtu[:, idx6]
    y = wbu.T @ hidq + wsu.T @ xtidx6g
    return y

@@ -1,0 +1,215 @@
+from contextlib import ExitStack
+
+import concourse.mybir as mybir
+
+K, J, R, T, F, C, S, N = 512, 512, 512, 1024, 1024, 1024, 256, 256
+FLOPS = 2 * K * R * J + 2 * R * N * C + 2 * K * N * C
+
+F32 = mybir.dt.float32
+BF16 = mybir.dt.bfloat16
+I32 = mybir.dt.int32
+U32 = mybir.dt.uint32
+U16 = mybir.dt.uint16
+U8 = mybir.dt.uint8
+FP8X4 = mybir.dt.float8_e4m3fn_x4
+FP4X4 = mybir.dt.float4_e2m1fn_x4
+ACT = mybir.ActivationFunctionType
+ALU = mybir.AluOpType
+
+P = 128
+PACK = 4
+PER_COL = 16
+FIRST_SLOTS = 128
+OUT_COLS = 256
+HALVES = N // P
+
+
+def tile_picked_tokens_store_one_overlay_further_plain_kernel(
+    tc, xt_words, xt_scales, wt_words, wt_scales, sa, wb_words, wb_scales, ws_words, ws_scales,
+    offs, offs2, offs3, offs4, offs5, offs6, out,
+):
+    nc = tc.nc
+
+    with ExitStack() as ctx:
+        keep = ctx.enter_context(tc.tile_pool(name="keep", bufs=1))
+        ring = ctx.enter_context(tc.tile_pool(name="ring", bufs=2))
+        psum = ctx.enter_context(tc.psum_pool(name="psum", bufs=1))
+
+        def load_list(src, name):
+            lst = keep.tile([P, src.shape[1]], U16, name=name)
+            nc.sync.dma_start(lst[:], src)
+            return lst
+
+        def cleared_plane(engine, width, name):
+            plane = keep.tile([P, width], U8, name=name, align_bytes=64)
+            engine.memset(plane[:].bitcast(I32), 0)
+            return plane
+
+        def load_plane(queue, plane, scales):
+            for q in range(4):
+                queue.dma_start(
+                    out=plane[32 * q : 32 * q + 4, :].bitcast(I32),
+                    in_=scales[0, 4 * q : 4 * q + 4, :].bitcast(I32),
+                )
+
+        def entries(lst, lo, hi):
+            return lst[:, lo // PER_COL : hi // PER_COL]
+
+        wt_plane = cleared_plane(nc.vector, F, "wt_plane")
+        xt_plane = cleared_plane(nc.vector, T, "xt_plane")
+        boards = [keep.tile([P, C], F32, name=f"board{i}") for i in range(2)]
+        overlay = keep.tile([P, C], F32)
+        nc.vector.memset(boards[0][:], 0.0)
+        nc.vector.memset(overlay[:], 0.0)
+        nc.gpsimd.memset(boards[1][:], 0.0)
+        ws_plane = cleared_plane(nc.gpsimd, N, "ws_plane")
+        wb_plane = cleared_plane(nc.gpsimd, N, "wb_plane")
+
+        feature_list = load_list(offs2, "feature_list")
+        wt_store = keep.tile([P, F], U16, align_bytes=64)
+        nc.sync.dma_start(out=wt_store[:].bitcast(I32), in_=wt_words[0].bitcast(I32))
+        load_plane(nc.sync, wt_plane, wt_scales)
+        slot_list = load_list(offs, "slot_list")
+        xt_store = keep.tile([P, T], U32, align_bytes=64)
+        nc.sync.dma_start(
+            out=xt_store[:].bitcast(I32), in_=xt_words[0].rearrange("p c b -> p (c b)").bitcast(I32)
+        )
+        load_plane(nc.sync, xt_plane, xt_scales)
+        board_list = load_list(offs3, "board_list")
+        pick_list = load_list(offs4, "pick_list")
+        weight = keep.tile([P, PACK], F32)
+        nc.gpsimd.dma_start(out=weight[:], in_=sa.rearrange("(p t) o -> p (t o)", t=PACK))
+        overlay_list = load_list(offs5, "overlay_list")
+        short_list = load_list(offs6, "short_list")
+        ws_codes = keep.tile([P, 2 * N], U8, align_bytes=64)
+        load_plane(nc.gpsimd, ws_plane, ws_scales)
+        nc.gpsimd.dma_start(out=ws_codes[:].bitcast(I32), in_=ws_words[0].bitcast(I32))
+        load_plane(nc.gpsimd, wb_plane, wb_scales)
+        wb_codes = keep.tile([P, N], U32, align_bytes=64)
+        nc.gpsimd.dma_start(
+            out=wb_codes[:].bitcast(I32), in_=wb_words[0].rearrange("p c b -> p (c b)").bitcast(I32)
+        )
+
+        wt_listed = keep.tile([P, R], U16, align_bytes=64)
+        wt_listed_scales = keep.tile([P, R], U8, align_bytes=64)
+        nc.vector.tensor_copy(wt_listed[:], wt_store[:].indirect(feature_list[:]))
+        nc.vector.tensor_copy(wt_listed_scales[:], wt_plane[:].indirect(feature_list[:]))
+
+        wt_dealt = keep.tile([P, PACK, P], U16, align_bytes=64)
+        wt_dealt_scales = keep.tile([P, PACK, P], U8, align_bytes=64)
+
+        def deal(t_lo, t_hi):
+            nc.vector.tensor_copy(
+                wt_dealt[:, t_lo:t_hi, :],
+                wt_listed[:].rearrange("p (m t) -> p t m", t=PACK)[:, t_lo:t_hi, :],
+            )
+            nc.vector.tensor_copy(
+                wt_dealt_scales[:, t_lo:t_hi, :],
+                wt_listed_scales[:].rearrange("p (m t) -> p t m", t=PACK)[:, t_lo:t_hi, :],
+            )
+
+        slot_codes = keep.tile([P, J], U32, tag="token_codes", align_bytes=64)
+        slot_scales = keep.tile([P, J], U8, tag="token_scales", align_bytes=64)
+        hidden = [keep.tile([P, J], F32, name=f"hidden{t}") for t in range(PACK)]
+
+        def first_product(t, cuts):
+            bank = psum.tile([P, J], F32, name="hidden_bank", bufs=4)
+            for lo, hi in zip(cuts[:-1], cuts[1:]):
+                nc.tensor.matmul_mx(
+                    out=bank[:, lo:hi],
+                    lhsT=wt_dealt[:, t, :].bitcast(FP4X4),
+                    lhsT_scale=wt_dealt_scales[:, t, :],
+                    rhs=slot_codes[:, lo:hi].bitcast(FP8X4),
+                    rhs_scale=slot_scales[:, lo:hi],
+                    start=True,
+                    stop=True,
+                )
+            return bank[:, cuts[0] : cuts[-1]]
+
+        def gather_tokens(codes, scales, lst, lo, hi):
+            nc.vector.tensor_copy(codes[:, lo:hi], xt_store[:].indirect(entries(lst, lo, hi)))
+            nc.vector.tensor_copy(scales[:, lo:hi], xt_plane[:].indirect(entries(lst, lo, hi)))
+
+        deal(0, 1)
+        gather_tokens(slot_codes, slot_scales, slot_list, 0, FIRST_SLOTS)
+        nc.scalar.copy(hidden[0][:, :FIRST_SLOTS], first_product(0, [0, FIRST_SLOTS]))
+        nc.scalar.activation(
+            boards[0][:].indirect(entries(board_list, 0, FIRST_SLOTS)), hidden[0][:, :FIRST_SLOTS], ACT.Copy
+        )
+        gather_tokens(slot_codes, slot_scales, slot_list, FIRST_SLOTS, J)
+        nc.vector.tensor_copy(hidden[0][:, FIRST_SLOTS:], first_product(0, [FIRST_SLOTS, J // 2, J]))
+        deal(1, PACK)
+        for t in range(1, PACK):
+            nc.vector.tensor_copy(hidden[t][:], first_product(t, [0, J]))
+
+        short_codes = keep.tile([P, C], U32, tag="token_codes", align_bytes=64)
+        short_scales = keep.tile([P, C], U8, tag="token_scales", align_bytes=64)
+        out_banks = [psum.tile([P, HALVES, OUT_COLS], F32, name=f"out_bank{b}") for b in range(C // OUT_COLS)]
+
+        def short_way(lo, hi):
+            gather_tokens(short_codes, short_scales, short_list, lo, hi)
+            for c0 in range(lo, hi, OUT_COLS):
+                for h in range(HALVES):
+                    nc.tensor.matmul_mx(
+                        out=out_banks[c0 // OUT_COLS][:, h, :],
+                        lhsT=ws_codes[:, 2 * P * h : 2 * P * (h + 1)].bitcast(FP4X4),
+                        lhsT_scale=ws_plane[:, P * h : P * (h + 1)],
+                        rhs=short_codes[:, c0 : c0 + OUT_COLS].bitcast(FP8X4),
+                        rhs_scale=short_scales[:, c0 : c0 + OUT_COLS],
+                        start=(h == 0),
+                        stop=False,
+                    )
+
+        stretches = [slice(c0, c0 + OUT_COLS) for c0 in range(0, C, OUT_COLS)]
+        diffs = [
+            [keep.tile([P, 2, OUT_COLS], F32, name=f"diffs{u}_{b}") for b in range(len(stretches))] for u in range(2)
+        ]
+        pairs = [keep.tile([P, 2, OUT_COLS, 2], BF16, name=f"pairs{b}", align_bytes=64) for b in range(len(stretches))]
+        last = PACK - 1
+
+        for t in range(PACK):
+            board = boards[t % 2]
+            picked = ring.tile([P, S], F32, name="picked")
+            nc.scalar.activation(
+                picked[:], hidden[t][:].indirect(pick_list[:]), ACT.Copy, scale=weight[:, t : t + 1]
+            )
+            lo = FIRST_SLOTS if t == 0 else 0
+            nc.scalar.activation(board[:].indirect(entries(board_list, lo, J)), hidden[t][:, lo:], ACT.Copy)
+            nc.scalar.activation(overlay[:].indirect(overlay_list[:]), picked[:], ACT.Copy)
+            if t < 2:
+                short_way(t * C // 2, (t + 1) * C // 2)
+            for b, cols in enumerate(stretches):
+                nc.vector.tensor_tensor(diffs[t // 2][b][:, t % 2, :], board[:, cols], overlay[:, cols], ALU.subtract)
+                side_by_side = diffs[t // 2][b][:].rearrange("p e c -> p c e")
+                if t == 1:
+                    nc.vector.scalar_tensor_tensor(
+                        out=pairs[b][:, 0], in0=side_by_side, scalar=-1.0, in1=side_by_side, op0=ALU.mult, op1=ALU.max
+                    )
+                if t == last:
+                    nc.scalar.activation(pairs[b][:, 1], side_by_side, ACT.Abs)
+
+        out_rows = out.rearrange("(h p) c -> p h c", p=P)
+        for b, cols in enumerate(stretches):
+            woven = keep.tile([P, OUT_COLS, 2], I32, name=f"woven{b}", align_bytes=64)
+            pair_words = pairs[b][:].rearrange("p u c e -> p (u c e)").bitcast(I32)
+            nc.vector.tensor_copy(woven[:], pair_words.rearrange("p (u c) -> p c u", u=2))
+            hid_codes = keep.tile([P, OUT_COLS], U32, name=f"hid_codes{b}", align_bytes=64)
+            hid_scales = keep.tile([P, OUT_COLS], U8, name=f"hid_scales{b}", align_bytes=64)
+            nc.vector.quantize_mx(
+                out=hid_codes[:].bitcast(FP8X4),
+                scales=hid_scales[:],
+                in_=woven[:].rearrange("p c u -> p (c u)").bitcast(BF16),
+            )
+            for h in range(HALVES):
+                nc.tensor.matmul_mx(
+                    out=out_banks[b][:, h, :],
+                    lhsT=wb_codes[:, P * h : P * (h + 1)].bitcast(FP8X4),
+                    lhsT_scale=wb_plane[:, P * h : P * (h + 1)],
+                    rhs=hid_codes[:].bitcast(FP8X4),
+                    rhs_scale=hid_scales[:],
+                    start=False,
+                    stop=(h == HALVES - 1),
+                )
+            result = keep.tile([P, HALVES, OUT_COLS], F32, name=f"result{b}")
+            nc.scalar.copy(result[:], out_banks[b][:])
+            nc.sync.dma_start(out=out_rows[:, :, cols], in_=result[:])

@@ -19,8 +19,8 @@ ALU = mybir.AluOpType
 P = 128
 PACK = 4
 PER_COL = 16
-FIRST_SLOTS = 128
-OUT_COLS = 256
+FIRST_SLOTS = 256
+OUT_CUTS = (0, 256, 512, 768, 896, 1024)
 HALVES = N // P
 
 
@@ -55,6 +55,8 @@ def tile_picked_tokens_store_one_overlay_further_plain_kernel(
         def entries(lst, lo, hi):
             return lst[:, lo // PER_COL : hi // PER_COL]
 
+        weight = keep.tile([P, PACK], F32)
+        nc.gpsimd.dma_start(out=weight[:], in_=sa.rearrange("(p t) o -> p (t o)", t=PACK))
         wt_plane = cleared_plane(nc.vector, F, "wt_plane")
         xt_plane = cleared_plane(nc.vector, T, "xt_plane")
         boards = [keep.tile([P, C], F32, name=f"board{i}") for i in range(2)]
@@ -77,16 +79,14 @@ def tile_picked_tokens_store_one_overlay_further_plain_kernel(
         load_plane(nc.sync, xt_plane, xt_scales)
         board_list = load_list(offs3, "board_list")
         pick_list = load_list(offs4, "pick_list")
-        weight = keep.tile([P, PACK], F32)
-        nc.gpsimd.dma_start(out=weight[:], in_=sa.rearrange("(p t) o -> p (t o)", t=PACK))
         overlay_list = load_list(offs5, "overlay_list")
         short_list = load_list(offs6, "short_list")
         ws_codes = keep.tile([P, 2 * N], U8, align_bytes=64)
-        load_plane(nc.gpsimd, ws_plane, ws_scales)
-        nc.gpsimd.dma_start(out=ws_codes[:].bitcast(I32), in_=ws_words[0].bitcast(I32))
-        load_plane(nc.gpsimd, wb_plane, wb_scales)
+        load_plane(nc.sync, ws_plane, ws_scales)
+        nc.sync.dma_start(out=ws_codes[:].bitcast(I32), in_=ws_words[0].bitcast(I32))
+        load_plane(nc.sync, wb_plane, wb_scales)
         wb_codes = keep.tile([P, N], U32, align_bytes=64)
-        nc.gpsimd.dma_start(
+        nc.sync.dma_start(
             out=wb_codes[:].bitcast(I32), in_=wb_words[0].rearrange("p c b -> p (c b)").bitcast(I32)
         )
 
@@ -95,30 +95,24 @@ def tile_picked_tokens_store_one_overlay_further_plain_kernel(
         nc.vector.tensor_copy(wt_listed[:], wt_store[:].indirect(feature_list[:]))
         nc.vector.tensor_copy(wt_listed_scales[:], wt_plane[:].indirect(feature_list[:]))
 
-        wt_dealt = keep.tile([P, PACK, P], U16, align_bytes=64)
-        wt_dealt_scales = keep.tile([P, PACK, P], U8, align_bytes=64)
-
-        def deal(t_lo, t_hi):
-            nc.vector.tensor_copy(
-                wt_dealt[:, t_lo:t_hi, :],
-                wt_listed[:].rearrange("p (m t) -> p t m", t=PACK)[:, t_lo:t_hi, :],
-            )
-            nc.vector.tensor_copy(
-                wt_dealt_scales[:, t_lo:t_hi, :],
-                wt_listed_scales[:].rearrange("p (m t) -> p t m", t=PACK)[:, t_lo:t_hi, :],
-            )
+        def deal(t):
+            codes = keep.tile([P, P], U16, name="dealt_codes", align_bytes=64)
+            scales = keep.tile([P, P], U8, name="dealt_scales", align_bytes=64)
+            nc.vector.tensor_copy(codes[:], wt_listed[:, t::PACK])
+            nc.vector.tensor_copy(scales[:], wt_listed_scales[:, t::PACK])
+            return codes, scales
 
         slot_codes = keep.tile([P, J], U32, tag="token_codes", align_bytes=64)
         slot_scales = keep.tile([P, J], U8, tag="token_scales", align_bytes=64)
         hidden = [keep.tile([P, J], F32, name=f"hidden{t}") for t in range(PACK)]
 
-        def first_product(t, cuts):
-            bank = psum.tile([P, J], F32, name="hidden_bank", bufs=4)
+        def first_product(dealt, cuts):
+            bank = psum.tile([P, J], F32, name="hidden_bank", bufs=3)
             for lo, hi in zip(cuts[:-1], cuts[1:]):
                 nc.tensor.matmul_mx(
                     out=bank[:, lo:hi],
-                    lhsT=wt_dealt[:, t, :].bitcast(FP4X4),
-                    lhsT_scale=wt_dealt_scales[:, t, :],
+                    lhsT=dealt[0][:].bitcast(FP4X4),
+                    lhsT_scale=dealt[1][:],
                     rhs=slot_codes[:, lo:hi].bitcast(FP8X4),
                     rhs_scale=slot_scales[:, lo:hi],
                     start=True,
@@ -126,45 +120,49 @@ def tile_picked_tokens_store_one_overlay_further_plain_kernel(
                 )
             return bank[:, cuts[0] : cuts[-1]]
 
-        def gather_tokens(codes, scales, lst, lo, hi):
+        def gather_codes(codes, lst, lo, hi):
             nc.vector.tensor_copy(codes[:, lo:hi], xt_store[:].indirect(entries(lst, lo, hi)))
+
+        def gather_scales(scales, lst, lo, hi):
             nc.vector.tensor_copy(scales[:, lo:hi], xt_plane[:].indirect(entries(lst, lo, hi)))
 
-        deal(0, 1)
-        gather_tokens(slot_codes, slot_scales, slot_list, 0, FIRST_SLOTS)
-        nc.scalar.copy(hidden[0][:, :FIRST_SLOTS], first_product(0, [0, FIRST_SLOTS]))
-        nc.scalar.activation(
-            boards[0][:].indirect(entries(board_list, 0, FIRST_SLOTS)), hidden[0][:, :FIRST_SLOTS], ACT.Copy
-        )
-        gather_tokens(slot_codes, slot_scales, slot_list, FIRST_SLOTS, J)
-        nc.vector.tensor_copy(hidden[0][:, FIRST_SLOTS:], first_product(0, [FIRST_SLOTS, J // 2, J]))
-        deal(1, PACK)
-        for t in range(1, PACK):
-            nc.vector.tensor_copy(hidden[t][:], first_product(t, [0, J]))
+        def to_board(t, lo, hi):
+            nc.scalar.activation(boards[t % 2][:].indirect(entries(board_list, lo, hi)), hidden[t][:, lo:hi], ACT.Copy)
 
+        dealt = deal(0)
+        gather_codes(slot_codes, slot_list, 0, J)
+        gather_scales(slot_scales, slot_list, 0, FIRST_SLOTS)
+        nc.scalar.copy(hidden[0][:, :FIRST_SLOTS], first_product(dealt, [0, FIRST_SLOTS]))
+        to_board(0, 0, FIRST_SLOTS)
+        gather_scales(slot_scales, slot_list, FIRST_SLOTS, J)
+        nc.vector.tensor_copy(hidden[0][:, FIRST_SLOTS:], first_product(dealt, [FIRST_SLOTS, J]))
+        for t in range(1, PACK):
+            nc.vector.tensor_copy(hidden[t][:], first_product(deal(t), [0, J]))
+
+        stretches = [slice(lo, hi) for lo, hi in zip(OUT_CUTS[:-1], OUT_CUTS[1:])]
+        widths = [cols.stop - cols.start for cols in stretches]
         short_codes = keep.tile([P, C], U32, tag="token_codes", align_bytes=64)
         short_scales = keep.tile([P, C], U8, tag="token_scales", align_bytes=64)
-        out_banks = [psum.tile([P, HALVES, OUT_COLS], F32, name=f"out_bank{b}") for b in range(C // OUT_COLS)]
+        out_banks = [psum.tile([P, HALVES, w], F32, name=f"out_bank{b}") for b, w in enumerate(widths)]
 
         def short_way(lo, hi):
-            gather_tokens(short_codes, short_scales, short_list, lo, hi)
-            for c0 in range(lo, hi, OUT_COLS):
-                for h in range(HALVES):
-                    nc.tensor.matmul_mx(
-                        out=out_banks[c0 // OUT_COLS][:, h, :],
-                        lhsT=ws_codes[:, 2 * P * h : 2 * P * (h + 1)].bitcast(FP4X4),
-                        lhsT_scale=ws_plane[:, P * h : P * (h + 1)],
-                        rhs=short_codes[:, c0 : c0 + OUT_COLS].bitcast(FP8X4),
-                        rhs_scale=short_scales[:, c0 : c0 + OUT_COLS],
-                        start=(h == 0),
-                        stop=False,
-                    )
+            gather_codes(short_codes, short_list, lo, hi)
+            gather_scales(short_scales, short_list, lo, hi)
+            for b, cols in enumerate(stretches):
+                if lo <= cols.start < hi:
+                    for h in range(HALVES):
+                        nc.tensor.matmul_mx(
+                            out=out_banks[b][:, h, :],
+                            lhsT=ws_codes[:, 2 * P * h : 2 * P * (h + 1)].bitcast(FP4X4),
+                            lhsT_scale=ws_plane[:, P * h : P * (h + 1)],
+                            rhs=short_codes[:, cols].bitcast(FP8X4),
+                            rhs_scale=short_scales[:, cols],
+                            start=(h == 0),
+                            stop=False,
+                        )
 
-        stretches = [slice(c0, c0 + OUT_COLS) for c0 in range(0, C, OUT_COLS)]
-        diffs = [
-            [keep.tile([P, 2, OUT_COLS], F32, name=f"diffs{u}_{b}") for b in range(len(stretches))] for u in range(2)
-        ]
-        pairs = [keep.tile([P, 2, OUT_COLS, 2], BF16, name=f"pairs{b}", align_bytes=64) for b in range(len(stretches))]
+        diffs = [[keep.tile([P, 2, w], F32, name=f"diffs{u}_{b}") for b, w in enumerate(widths)] for u in range(2)]
+        pairs = [keep.tile([P, 2, w, 2], BF16, name=f"pairs{b}", align_bytes=64) for b, w in enumerate(widths)]
         last = PACK - 1
 
         for t in range(PACK):
@@ -173,8 +171,7 @@ def tile_picked_tokens_store_one_overlay_further_plain_kernel(
             nc.scalar.activation(
                 picked[:], hidden[t][:].indirect(pick_list[:]), ACT.Copy, scale=weight[:, t : t + 1]
             )
-            lo = FIRST_SLOTS if t == 0 else 0
-            nc.scalar.activation(board[:].indirect(entries(board_list, lo, J)), hidden[t][:, lo:], ACT.Copy)
+            to_board(t, FIRST_SLOTS if t == 0 else 0, J)
             nc.scalar.activation(overlay[:].indirect(overlay_list[:]), picked[:], ACT.Copy)
             if t < 2:
                 short_way(t * C // 2, (t + 1) * C // 2)
@@ -190,11 +187,11 @@ def tile_picked_tokens_store_one_overlay_further_plain_kernel(
 
         out_rows = out.rearrange("(h p) c -> p h c", p=P)
         for b, cols in enumerate(stretches):
-            woven = keep.tile([P, OUT_COLS, 2], I32, name=f"woven{b}", align_bytes=64)
+            woven = keep.tile([P, widths[b], 2], I32, name=f"woven{b}", align_bytes=64)
             pair_words = pairs[b][:].rearrange("p u c e -> p (u c e)").bitcast(I32)
             nc.vector.tensor_copy(woven[:], pair_words.rearrange("p (u c) -> p c u", u=2))
-            hid_codes = keep.tile([P, OUT_COLS], U32, name=f"hid_codes{b}", align_bytes=64)
-            hid_scales = keep.tile([P, OUT_COLS], U8, name=f"hid_scales{b}", align_bytes=64)
+            hid_codes = keep.tile([P, widths[b]], U32, name=f"hid_codes{b}", align_bytes=64)
+            hid_scales = keep.tile([P, widths[b]], U8, name=f"hid_scales{b}", align_bytes=64)
             nc.vector.quantize_mx(
                 out=hid_codes[:].bitcast(FP8X4),
                 scales=hid_scales[:],
@@ -210,6 +207,9 @@ def tile_picked_tokens_store_one_overlay_further_plain_kernel(
                     start=False,
                     stop=(h == HALVES - 1),
                 )
-            result = keep.tile([P, HALVES, OUT_COLS], F32, name=f"result{b}")
-            nc.scalar.copy(result[:], out_banks[b][:])
+            result = keep.tile([P, HALVES, widths[b]], F32, name=f"result{b}")
+            if widths[b] == max(widths):
+                nc.scalar.copy(result[:], out_banks[b][:])
+            else:
+                nc.vector.tensor_copy(result[:], out_banks[b][:])
             nc.sync.dma_start(out=out_rows[:, :, cols], in_=result[:])

@@ -19,8 +19,9 @@ ALU = mybir.AluOpType
 P = 128
 PACK = 4
 PER_COL = 16
-FIRST_SLOTS = 256
+FIRST_CUTS = (0, 256, 512)
 OUT_CUTS = (0, 256, 512, 768, 896, 1024)
+LATE_COLS = 768
 HALVES = N // P
 
 
@@ -55,31 +56,30 @@ def tile_picked_tokens_store_one_overlay_further_plain_kernel(
         def entries(lst, lo, hi):
             return lst[:, lo // PER_COL : hi // PER_COL]
 
-        weight = keep.tile([P, PACK], F32)
-        nc.gpsimd.dma_start(out=weight[:], in_=sa.rearrange("(p t) o -> p (t o)", t=PACK))
         wt_plane = cleared_plane(nc.vector, F, "wt_plane")
         xt_plane = cleared_plane(nc.vector, T, "xt_plane")
-        boards = [keep.tile([P, C], F32, name=f"board{i}") for i in range(2)]
+        boards = [keep.tile([P, C], F32, name="board0", align_bytes=64)]
         overlay = keep.tile([P, C], F32)
         nc.vector.memset(boards[0][:], 0.0)
         nc.vector.memset(overlay[:], 0.0)
-        nc.gpsimd.memset(boards[1][:], 0.0)
         ws_plane = cleared_plane(nc.gpsimd, N, "ws_plane")
         wb_plane = cleared_plane(nc.gpsimd, N, "wb_plane")
 
-        feature_list = load_list(offs2, "feature_list")
         wt_store = keep.tile([P, F], U16, align_bytes=64)
         nc.sync.dma_start(out=wt_store[:].bitcast(I32), in_=wt_words[0].bitcast(I32))
+        feature_list = load_list(offs2, "feature_list")
         load_plane(nc.sync, wt_plane, wt_scales)
         slot_list = load_list(offs, "slot_list")
         xt_store = keep.tile([P, T], U32, align_bytes=64)
         nc.sync.dma_start(
             out=xt_store[:].bitcast(I32), in_=xt_words[0].rearrange("p c b -> p (c b)").bitcast(I32)
         )
-        load_plane(nc.sync, xt_plane, xt_scales)
         board_list = load_list(offs3, "board_list")
         pick_list = load_list(offs4, "pick_list")
+        weight = keep.tile([P, PACK], F32)
+        nc.sync.dma_start(out=weight[:], in_=sa.rearrange("(p t) o -> p (t o)", t=PACK))
         overlay_list = load_list(offs5, "overlay_list")
+        load_plane(nc.sync, xt_plane, xt_scales)
         short_list = load_list(offs6, "short_list")
         ws_codes = keep.tile([P, 2 * N], U8, align_bytes=64)
         load_plane(nc.sync, ws_plane, ws_scales)
@@ -90,29 +90,31 @@ def tile_picked_tokens_store_one_overlay_further_plain_kernel(
             out=wb_codes[:].bitcast(I32), in_=wb_words[0].rearrange("p c b -> p (c b)").bitcast(I32)
         )
 
-        wt_listed = keep.tile([P, R], U16, align_bytes=64)
+        wt_listed = keep.tile([P, R], U16, tag="listed_then_board", align_bytes=64)
         wt_listed_scales = keep.tile([P, R], U8, align_bytes=64)
         nc.vector.tensor_copy(wt_listed[:], wt_store[:].indirect(feature_list[:]))
         nc.vector.tensor_copy(wt_listed_scales[:], wt_plane[:].indirect(feature_list[:]))
 
-        def deal(t):
-            codes = keep.tile([P, P], U16, name="dealt_codes", align_bytes=64)
-            scales = keep.tile([P, P], U8, name="dealt_scales", align_bytes=64)
-            nc.vector.tensor_copy(codes[:], wt_listed[:, t::PACK])
-            nc.vector.tensor_copy(scales[:], wt_listed_scales[:, t::PACK])
-            return codes, scales
+        def deal(t_lo, t_hi):
+            count = t_hi - t_lo
+            codes = keep.tile([P, count, P], U16, name="dealt_codes", tag="dealt_then_diffs", align_bytes=64)
+            scales = keep.tile([P, count, P], U8, name="dealt_scales", align_bytes=64)
+            nc.vector.tensor_copy(codes[:], wt_listed[:].rearrange("p (m t) -> p t m", t=PACK)[:, t_lo:t_hi, :])
+            nc.vector.tensor_copy(scales[:], wt_listed_scales[:].rearrange("p (m t) -> p t m", t=PACK)[:, t_lo:t_hi, :])
+            return [(codes[:, i, :], scales[:, i, :]) for i in range(count)]
 
         slot_codes = keep.tile([P, J], U32, tag="token_codes", align_bytes=64)
         slot_scales = keep.tile([P, J], U8, tag="token_scales", align_bytes=64)
-        hidden = [keep.tile([P, J], F32, name=f"hidden{t}") for t in range(PACK)]
+        hidden = {t: keep.tile([P, J], F32, name=f"hidden{t}") for t in range(2, PACK)}
+        hidden[0] = keep.tile([P, J], F32, name="hidden0", tag="first_hidden")
 
         def first_product(dealt, cuts):
-            bank = psum.tile([P, J], F32, name="hidden_bank", bufs=3)
+            bank = psum.tile([P, J], F32, name="hidden_bank", bufs=2)
             for lo, hi in zip(cuts[:-1], cuts[1:]):
                 nc.tensor.matmul_mx(
                     out=bank[:, lo:hi],
-                    lhsT=dealt[0][:].bitcast(FP4X4),
-                    lhsT_scale=dealt[1][:],
+                    lhsT=dealt[0].bitcast(FP4X4),
+                    lhsT_scale=dealt[1],
                     rhs=slot_codes[:, lo:hi].bitcast(FP8X4),
                     rhs_scale=slot_scales[:, lo:hi],
                     start=True,
@@ -126,28 +128,34 @@ def tile_picked_tokens_store_one_overlay_further_plain_kernel(
         def gather_scales(scales, lst, lo, hi):
             nc.vector.tensor_copy(scales[:, lo:hi], xt_plane[:].indirect(entries(lst, lo, hi)))
 
-        def to_board(t, lo, hi):
-            nc.scalar.activation(boards[t % 2][:].indirect(entries(board_list, lo, hi)), hidden[t][:, lo:hi], ACT.Copy)
+        def to_board(t, values, lo, hi):
+            nc.scalar.activation(boards[t % 2][:].indirect(entries(board_list, lo, hi)), values, ACT.Copy)
 
-        dealt = deal(0)
+        dealt = deal(0, 1)[0]
         gather_codes(slot_codes, slot_list, 0, J)
-        gather_scales(slot_scales, slot_list, 0, FIRST_SLOTS)
-        nc.scalar.copy(hidden[0][:, :FIRST_SLOTS], first_product(dealt, [0, FIRST_SLOTS]))
-        to_board(0, 0, FIRST_SLOTS)
-        gather_scales(slot_scales, slot_list, FIRST_SLOTS, J)
-        nc.vector.tensor_copy(hidden[0][:, FIRST_SLOTS:], first_product(dealt, [FIRST_SLOTS, J]))
-        for t in range(1, PACK):
-            nc.vector.tensor_copy(hidden[t][:], first_product(deal(t), [0, J]))
+        for lo, hi in zip(FIRST_CUTS[:-1], FIRST_CUTS[1:]):
+            gather_scales(slot_scales, slot_list, lo, hi)
+            sums = first_product(dealt, [lo, hi])
+            if lo == 0:
+                nc.scalar.copy(hidden[0][:, lo:hi], sums)
+            else:
+                nc.vector.tensor_copy(hidden[0][:, lo:hi], sums)
+            if hi < J:
+                to_board(0, hidden[0][:, lo:hi], lo, hi)
+        rest = deal(1, PACK)
+        held_sums = first_product(rest[0], [0, J])
+        nc.vector.tensor_copy(hidden[2][:], first_product(rest[1], [0, J]))
+        boards.append(keep.tile([P, C], F32, name="board1", tag="listed_then_board", align_bytes=64))
+        nc.vector.memset(boards[1][:], 0.0)
 
         stretches = [slice(lo, hi) for lo, hi in zip(OUT_CUTS[:-1], OUT_CUTS[1:])]
         widths = [cols.stop - cols.start for cols in stretches]
         short_codes = keep.tile([P, C], U32, tag="token_codes", align_bytes=64)
-        short_scales = keep.tile([P, C], U8, tag="token_scales", align_bytes=64)
         out_banks = [psum.tile([P, HALVES, w], F32, name=f"out_bank{b}") for b, w in enumerate(widths)]
 
-        def short_way(lo, hi):
-            gather_codes(short_codes, short_list, lo, hi)
-            gather_scales(short_scales, short_list, lo, hi)
+        def short_way(lo, hi, tag):
+            short_scales = keep.tile([P, hi - lo], U8, name="short_scales", tag=tag, align_bytes=64)
+            nc.vector.tensor_copy(short_scales[:], xt_plane[:].indirect(entries(short_list, lo, hi)))
             for b, cols in enumerate(stretches):
                 if lo <= cols.start < hi:
                     for h in range(HALVES):
@@ -156,12 +164,14 @@ def tile_picked_tokens_store_one_overlay_further_plain_kernel(
                             lhsT=ws_codes[:, 2 * P * h : 2 * P * (h + 1)].bitcast(FP4X4),
                             lhsT_scale=ws_plane[:, P * h : P * (h + 1)],
                             rhs=short_codes[:, cols].bitcast(FP8X4),
-                            rhs_scale=short_scales[:, cols],
+                            rhs_scale=short_scales[:, cols.start - lo : cols.stop - lo],
                             start=(h == 0),
                             stop=False,
                         )
 
-        diffs = [[keep.tile([P, 2, w], F32, name=f"diffs{u}_{b}") for b, w in enumerate(widths)] for u in range(2)]
+        early_diffs = keep.tile([P, 2, C], F32, tag="dealt_then_diffs", align_bytes=64)
+        third_diff = keep.tile([P, C], F32)
+        last_diffs = [keep.tile([P, w], F32, name=f"last_diffs{b}") for b, w in enumerate(widths)]
         pairs = [keep.tile([P, 2, w, 2], BF16, name=f"pairs{b}", align_bytes=64) for b, w in enumerate(widths)]
         last = PACK - 1
 
@@ -171,19 +181,36 @@ def tile_picked_tokens_store_one_overlay_further_plain_kernel(
             nc.scalar.activation(
                 picked[:], hidden[t][:].indirect(pick_list[:]), ACT.Copy, scale=weight[:, t : t + 1]
             )
-            to_board(t, FIRST_SLOTS if t == 0 else 0, J)
+            lo = FIRST_CUTS[-2] if t == 0 else 0
+            to_board(t, hidden[t][:, lo:], lo, J)
+            if t == 0:
+                hidden[1] = keep.tile([P, J], F32, name="hidden1", tag="first_hidden")
+                nc.vector.tensor_copy(hidden[1][:], held_sums)
+                nc.vector.tensor_copy(hidden[3][:], first_product(rest[2], [0, J]))
             nc.scalar.activation(overlay[:].indirect(overlay_list[:]), picked[:], ACT.Copy)
             if t < 2:
-                short_way(t * C // 2, (t + 1) * C // 2)
+                nc.vector.tensor_tensor(early_diffs[:, t, :], board[:], overlay[:], ALU.subtract)
+                gather_codes(short_codes, short_list, (1 - t) * C // 2, (2 - t) * C // 2)
+            if t == 0:
+                short_way(LATE_COLS, C, "token_scales")
+            if t == last:
+                short_way(0, LATE_COLS, "board0")
+            if t == 2:
+                nc.vector.tensor_tensor(third_diff[:], board[:], overlay[:], ALU.subtract)
             for b, cols in enumerate(stretches):
-                nc.vector.tensor_tensor(diffs[t // 2][b][:, t % 2, :], board[:, cols], overlay[:, cols], ALU.subtract)
-                side_by_side = diffs[t // 2][b][:].rearrange("p e c -> p c e")
                 if t == 1:
+                    side_by_side = early_diffs[:, :, cols].rearrange("p e c -> p c e")
                     nc.vector.scalar_tensor_tensor(
                         out=pairs[b][:, 0], in0=side_by_side, scalar=-1.0, in1=side_by_side, op0=ALU.mult, op1=ALU.max
                     )
+                if t == 2:
+                    nc.vector.scalar_tensor_tensor(
+                        out=pairs[b][:, 1, :, 0], in0=third_diff[:, cols], scalar=-1.0, in1=third_diff[:, cols],
+                        op0=ALU.mult, op1=ALU.max,
+                    )
                 if t == last:
-                    nc.scalar.activation(pairs[b][:, 1], side_by_side, ACT.Abs)
+                    nc.vector.tensor_tensor(last_diffs[b][:], board[:, cols], overlay[:, cols], ALU.subtract)
+                    nc.scalar.activation(pairs[b][:, 1, :, 1], last_diffs[b][:], ACT.Abs)
 
         out_rows = out.rearrange("(h p) c -> p h c", p=P)
         for b, cols in enumerate(stretches):
@@ -208,8 +235,5 @@ def tile_picked_tokens_store_one_overlay_further_plain_kernel(
                     stop=(h == HALVES - 1),
                 )
             result = keep.tile([P, HALVES, widths[b]], F32, name=f"result{b}")
-            if widths[b] == max(widths):
-                nc.scalar.copy(result[:], out_banks[b][:])
-            else:
-                nc.vector.tensor_copy(result[:], out_banks[b][:])
+            nc.scalar.copy(result[:], out_banks[b][:])
             nc.sync.dma_start(out=out_rows[:, :, cols], in_=result[:])

from contextlib import ExitStack

import concourse.mybir as mybir

K, J, R, T, F, C, S, N = 512, 512, 512, 1024, 1024, 1024, 256, 256
FLOPS = 2 * K * R * J + 2 * R * N * C + 2 * K * N * C

F32 = mybir.dt.float32
BF16 = mybir.dt.bfloat16
I32 = mybir.dt.int32
U32 = mybir.dt.uint32
U16 = mybir.dt.uint16
U8 = mybir.dt.uint8
FP8X4 = mybir.dt.float8_e4m3fn_x4
FP4X4 = mybir.dt.float4_e2m1fn_x4
ACT = mybir.ActivationFunctionType
ALU = mybir.AluOpType

P = 128
PACK = 4
PER_COL = 16
FIRST_CUTS = (0, 256, 512)
OUT_CUTS = (0, 256, 512, 768, 896, 1024)
LATE_COLS = 768
HALVES = N // P


def tile_picked_tokens_store_one_overlay_further_plain_kernel(
    tc, xt_words, xt_scales, wt_words, wt_scales, sa, wb_words, wb_scales, ws_words, ws_scales,
    offs, offs2, offs3, offs4, offs5, offs6, out,
):
    nc = tc.nc

    with ExitStack() as ctx:
        keep = ctx.enter_context(tc.tile_pool(name="keep", bufs=1))
        ring = ctx.enter_context(tc.tile_pool(name="ring", bufs=2))
        psum = ctx.enter_context(tc.psum_pool(name="psum", bufs=1))

        def load_list(src, name):
            lst = keep.tile([P, src.shape[1]], U16, name=name)
            nc.sync.dma_start(lst[:], src)
            return lst

        def cleared_plane(engine, width, name):
            plane = keep.tile([P, width], U8, name=name, align_bytes=64)
            engine.memset(plane[:].bitcast(I32), 0)
            return plane

        def load_plane(queue, plane, scales):
            for q in range(4):
                queue.dma_start(
                    out=plane[32 * q : 32 * q + 4, :].bitcast(I32),
                    in_=scales[0, 4 * q : 4 * q + 4, :].bitcast(I32),
                )

        def entries(lst, lo, hi):
            return lst[:, lo // PER_COL : hi // PER_COL]

        wt_plane = cleared_plane(nc.vector, F, "wt_plane")
        xt_plane = cleared_plane(nc.vector, T, "xt_plane")
        boards = [keep.tile([P, C], F32, name="board0", align_bytes=64)]
        overlay = keep.tile([P, C], F32)
        nc.vector.memset(boards[0][:], 0.0)
        nc.vector.memset(overlay[:], 0.0)
        ws_plane = cleared_plane(nc.gpsimd, N, "ws_plane")
        wb_plane = cleared_plane(nc.gpsimd, N, "wb_plane")

        wt_store = keep.tile([P, F], U16, align_bytes=64)
        nc.sync.dma_start(out=wt_store[:].bitcast(I32), in_=wt_words[0].bitcast(I32))
        feature_list = load_list(offs2, "feature_list")
        load_plane(nc.sync, wt_plane, wt_scales)
        slot_list = load_list(offs, "slot_list")
        xt_store = keep.tile([P, T], U32, align_bytes=64)
        nc.sync.dma_start(
            out=xt_store[:].bitcast(I32), in_=xt_words[0].rearrange("p c b -> p (c b)").bitcast(I32)
        )
        board_list = load_list(offs3, "board_list")
        pick_list = load_list(offs4, "pick_list")
        weight = keep.tile([P, PACK], F32)
        nc.sync.dma_start(out=weight[:], in_=sa.rearrange("(p t) o -> p (t o)", t=PACK))
        overlay_list = load_list(offs5, "overlay_list")
        load_plane(nc.sync, xt_plane, xt_scales)
        short_list = load_list(offs6, "short_list")
        ws_codes = keep.tile([P, 2 * N], U8, align_bytes=64)
        load_plane(nc.sync, ws_plane, ws_scales)
        nc.sync.dma_start(out=ws_codes[:].bitcast(I32), in_=ws_words[0].bitcast(I32))
        load_plane(nc.sync, wb_plane, wb_scales)
        wb_codes = keep.tile([P, N], U32, align_bytes=64)
        nc.sync.dma_start(
            out=wb_codes[:].bitcast(I32), in_=wb_words[0].rearrange("p c b -> p (c b)").bitcast(I32)
        )

        wt_listed = keep.tile([P, R], U16, tag="listed_then_board", align_bytes=64)
        wt_listed_scales = keep.tile([P, R], U8, align_bytes=64)
        nc.vector.tensor_copy(wt_listed[:], wt_store[:].indirect(feature_list[:]))
        nc.vector.tensor_copy(wt_listed_scales[:], wt_plane[:].indirect(feature_list[:]))

        def deal(t_lo, t_hi):
            count = t_hi - t_lo
            codes = keep.tile([P, count, P], U16, name="dealt_codes", tag="dealt_then_diffs", align_bytes=64)
            scales = keep.tile([P, count, P], U8, name="dealt_scales", align_bytes=64)
            nc.vector.tensor_copy(codes[:], wt_listed[:].rearrange("p (m t) -> p t m", t=PACK)[:, t_lo:t_hi, :])
            nc.vector.tensor_copy(scales[:], wt_listed_scales[:].rearrange("p (m t) -> p t m", t=PACK)[:, t_lo:t_hi, :])
            return [(codes[:, i, :], scales[:, i, :]) for i in range(count)]

        slot_codes = keep.tile([P, J], U32, tag="token_codes", align_bytes=64)
        slot_scales = keep.tile([P, J], U8, tag="token_scales", align_bytes=64)
        hidden = {t: keep.tile([P, J], F32, name=f"hidden{t}") for t in range(2, PACK)}
        hidden[0] = keep.tile([P, J], F32, name="hidden0", tag="first_hidden")

        def first_product(dealt, cuts):
            bank = psum.tile([P, J], F32, name="hidden_bank", bufs=2)
            for lo, hi in zip(cuts[:-1], cuts[1:]):
                nc.tensor.matmul_mx(
                    out=bank[:, lo:hi],
                    lhsT=dealt[0].bitcast(FP4X4),
                    lhsT_scale=dealt[1],
                    rhs=slot_codes[:, lo:hi].bitcast(FP8X4),
                    rhs_scale=slot_scales[:, lo:hi],
                    start=True,
                    stop=True,
                )
            return bank[:, cuts[0] : cuts[-1]]

        def gather_codes(codes, lst, lo, hi):
            nc.vector.tensor_copy(codes[:, lo:hi], xt_store[:].indirect(entries(lst, lo, hi)))

        def gather_scales(scales, lst, lo, hi):
            nc.vector.tensor_copy(scales[:, lo:hi], xt_plane[:].indirect(entries(lst, lo, hi)))

        def to_board(t, values, lo, hi):
            nc.scalar.activation(boards[t % 2][:].indirect(entries(board_list, lo, hi)), values, ACT.Copy)

        dealt = deal(0, 1)[0]
        gather_codes(slot_codes, slot_list, 0, J)
        for lo, hi in zip(FIRST_CUTS[:-1], FIRST_CUTS[1:]):
            gather_scales(slot_scales, slot_list, lo, hi)
            sums = first_product(dealt, [lo, hi])
            if lo == 0:
                nc.scalar.copy(hidden[0][:, lo:hi], sums)
            else:
                nc.vector.tensor_copy(hidden[0][:, lo:hi], sums)
            if hi < J:
                to_board(0, hidden[0][:, lo:hi], lo, hi)
        rest = deal(1, PACK)
        held_sums = first_product(rest[0], [0, J])
        nc.vector.tensor_copy(hidden[2][:], first_product(rest[1], [0, J]))
        boards.append(keep.tile([P, C], F32, name="board1", tag="listed_then_board", align_bytes=64))
        nc.vector.memset(boards[1][:], 0.0)

        stretches = [slice(lo, hi) for lo, hi in zip(OUT_CUTS[:-1], OUT_CUTS[1:])]
        widths = [cols.stop - cols.start for cols in stretches]
        short_codes = keep.tile([P, C], U32, tag="token_codes", align_bytes=64)
        out_banks = [psum.tile([P, HALVES, w], F32, name=f"out_bank{b}") for b, w in enumerate(widths)]

        def short_way(lo, hi, tag):
            short_scales = keep.tile([P, hi - lo], U8, name="short_scales", tag=tag, align_bytes=64)
            nc.vector.tensor_copy(short_scales[:], xt_plane[:].indirect(entries(short_list, lo, hi)))
            for b, cols in enumerate(stretches):
                if lo <= cols.start < hi:
                    for h in range(HALVES):
                        nc.tensor.matmul_mx(
                            out=out_banks[b][:, h, :],
                            lhsT=ws_codes[:, 2 * P * h : 2 * P * (h + 1)].bitcast(FP4X4),
                            lhsT_scale=ws_plane[:, P * h : P * (h + 1)],
                            rhs=short_codes[:, cols].bitcast(FP8X4),
                            rhs_scale=short_scales[:, cols.start - lo : cols.stop - lo],
                            start=(h == 0),
                            stop=False,
                        )

        early_diffs = keep.tile([P, 2, C], F32, tag="dealt_then_diffs", align_bytes=64)
        third_diff = keep.tile([P, C], F32)
        last_diffs = [keep.tile([P, w], F32, name=f"last_diffs{b}") for b, w in enumerate(widths)]
        pairs = [keep.tile([P, 2, w, 2], BF16, name=f"pairs{b}", align_bytes=64) for b, w in enumerate(widths)]
        last = PACK - 1

        for t in range(PACK):
            board = boards[t % 2]
            picked = ring.tile([P, S], F32, name="picked")
            nc.scalar.activation(
                picked[:], hidden[t][:].indirect(pick_list[:]), ACT.Copy, scale=weight[:, t : t + 1]
            )
            lo = FIRST_CUTS[-2] if t == 0 else 0
            to_board(t, hidden[t][:, lo:], lo, J)
            if t == 0:
                hidden[1] = keep.tile([P, J], F32, name="hidden1", tag="first_hidden")
                nc.vector.tensor_copy(hidden[1][:], held_sums)
                nc.vector.tensor_copy(hidden[3][:], first_product(rest[2], [0, J]))
            nc.scalar.activation(overlay[:].indirect(overlay_list[:]), picked[:], ACT.Copy)
            if t < 2:
                nc.vector.tensor_tensor(early_diffs[:, t, :], board[:], overlay[:], ALU.subtract)
                gather_codes(short_codes, short_list, (1 - t) * C // 2, (2 - t) * C // 2)
            if t == 0:
                short_way(LATE_COLS, C, "token_scales")
            if t == last:
                short_way(0, LATE_COLS, "board0")
            if t == 2:
                nc.vector.tensor_tensor(third_diff[:], board[:], overlay[:], ALU.subtract)
            for b, cols in enumerate(stretches):
                if t == 1:
                    side_by_side = early_diffs[:, :, cols].rearrange("p e c -> p c e")
                    nc.vector.scalar_tensor_tensor(
                        out=pairs[b][:, 0], in0=side_by_side, scalar=-1.0, in1=side_by_side, op0=ALU.mult, op1=ALU.max
                    )
                if t == 2:
                    nc.vector.scalar_tensor_tensor(
                        out=pairs[b][:, 1, :, 0], in0=third_diff[:, cols], scalar=-1.0, in1=third_diff[:, cols],
                        op0=ALU.mult, op1=ALU.max,
                    )
                if t == last:
                    nc.vector.tensor_tensor(last_diffs[b][:], board[:, cols], overlay[:, cols], ALU.subtract)
                    nc.scalar.activation(pairs[b][:, 1, :, 1], last_diffs[b][:], ACT.Abs)

        out_rows = out.rearrange("(h p) c -> p h c", p=P)
        for b, cols in enumerate(stretches):
            woven = keep.tile([P, widths[b], 2], I32, name=f"woven{b}", align_bytes=64)
            pair_words = pairs[b][:].rearrange("p u c e -> p (u c e)").bitcast(I32)
            nc.vector.tensor_copy(woven[:], pair_words.rearrange("p (u c) -> p c u", u=2))
            hid_codes = keep.tile([P, widths[b]], U32, name=f"hid_codes{b}", align_bytes=64)
            hid_scales = keep.tile([P, widths[b]], U8, name=f"hid_scales{b}", align_bytes=64)
            nc.vector.quantize_mx(
                out=hid_codes[:].bitcast(FP8X4),
                scales=hid_scales[:],
                in_=woven[:].rearrange("p c u -> p (c u)").bitcast(BF16),
            )
            for h in range(HALVES):
                nc.tensor.matmul_mx(
                    out=out_banks[b][:, h, :],
                    lhsT=wb_codes[:, P * h : P * (h + 1)].bitcast(FP8X4),
                    lhsT_scale=wb_plane[:, P * h : P * (h + 1)],
                    rhs=hid_codes[:].bitcast(FP8X4),
                    rhs_scale=hid_scales[:],
                    start=False,
                    stop=(h == HALVES - 1),
                )
            result = keep.tile([P, HALVES, widths[b]], F32, name=f"result{b}")
            nc.scalar.copy(result[:], out_banks[b][:])
            nc.sync.dma_start(out=out_rows[:, :, cols], in_=result[:])
